import numpy as np
import ml_dtypes


def mxq(x, axis, fmt="e4m3"):
    dtype, down = {"e4m3": (ml_dtypes.float8_e4m3fn, 7), "e5m2": (ml_dtypes.float8_e5m2, 14)}[fmt]
    v = np.moveaxis(np.asarray(x, np.float32).astype(ml_dtypes.bfloat16).astype(np.float64), axis, -1)
    blocks = v.reshape(v.shape[:-1] + (-1, 32))
    amax = np.abs(blocks).max(-1, keepdims=True)
    byte = np.maximum(np.where(amax > 0, np.frexp(amax)[1] - 1 + 127, 0) - down, 1)
    scale = np.exp2(byte - 127.0)
    codes = (blocks / scale).astype(np.float32).astype(dtype).astype(np.float64)
    return np.moveaxis((codes * scale).reshape(v.shape), -1, axis)


WIDE = False


def mx_kscale(k):
    if not WIDE:
        return np.ones(k)
    levels = np.array([10, -10, 5, -5, 0])
    if k % 512:
        return np.exp2(np.random.permutation(np.resize(levels, k // 32))).repeat(32)
    a = np.empty((k // 512, 16))
    for p in range(k // 512):
        a[p, :8] = np.random.permutation(np.resize(levels, 8))
        for g in range(8):
            far = levels[np.abs(levels - a[p, g]) >= 10]
            a[p, g + 8] = far[np.random.randint(len(far))]
    return np.exp2(a.ravel()).repeat(32)


def f64(x):
    return np.asarray(x).astype(np.float64)


def striped(idx):
    return np.tile(idx.reshape(-1, 16).T, (8, 1)).astype(np.uint16)


def unstriped(offs):
    return offs[:16].T.reshape(-1).astype(np.int64)


def striped8(idx):
    return np.concatenate([x.reshape(-1, 16).T for x in idx]).astype(np.uint16)


def runs(offs, k):
    lists = np.stack([offs[16 * r : 16 * r + 16].T.reshape(-1) for r in range(8)]).astype(np.int64)
    return lists[np.arange(k) % 512 // 64]


def pack_weight(w):
    k, n = w.shape
    w = f64(np.asarray(w, np.float32).astype(ml_dtypes.bfloat16)).reshape(k // 32, 32, n)
    amax = np.abs(w).max(1)
    byte = np.clip(np.where(amax > 0, np.frexp(amax)[1] - 1 + 127 - 7, 1), 1, 254)
    scaled = (w * np.exp2(127.0 - byte)[:, None, :]).reshape(k, n).astype(np.float32)
    words = np.ascontiguousarray(scaled.reshape(k // 512, 128, 4, n).transpose(0, 1, 3, 2)).astype(ml_dtypes.float8_e4m3fn).view(np.uint8)
    return words, np.ascontiguousarray(byte.astype(np.uint8).reshape(k // 512, 16, n))


def unpack_weight(words, scales):
    g, p, n, _ = words.shape
    vals = np.ascontiguousarray(words).view(ml_dtypes.float8_e4m3fn).astype(np.float64) * np.repeat(np.exp2(scales.astype(np.float64) - 127.0), 8, axis=1)[..., None]
    return vals.transpose(0, 1, 3, 2).reshape(g * 512, n)


K, T, S, G, H = 512, 1024, 512, 2048, 512


def setup_inputs():
    n = np.random.standard_normal
    s = mx_kscale(K)[:, None]
    packed_xT = pack_weight(n((K, T)) * s)
    packed_dT = pack_weight(n((K, G)) / s)
    return {
        "x_words": packed_xT[0],
        "x_scales": packed_xT[1],
        "d_words": packed_dT[0],
        "d_scales": packed_dT[1],
        "gs": (np.random.uniform(0.5, 1.5, (K, 1)) * s).astype(np.float32),
        "offs": striped(np.random.permutation(T)[:S]),
        "k1": striped8(np.random.randint(0, G, (8, H))),
        "n1": striped8(np.stack([np.random.permutation(S) for _ in range(8)])),
        "n2": striped8(np.stack([np.random.permutation(S) for _ in range(8)])),
        "k2": striped8(np.random.randint(0, G, (8, H))),
        "n3": striped8(np.stack([np.random.permutation(S) for _ in range(8)])),
    }


def reference(x_words, x_scales, d_words, d_scales, gs, offs, k1, n1, n2, k2, n3):
    d_k2 = unpack_weight(d_words, d_scales)[np.arange(K)[:, None], runs(k2, K)]
    d_k1 = unpack_weight(d_words, d_scales)[np.arange(K)[:, None], runs(k1, K)]
    xq = unpack_weight(x_words, x_scales)[:, unstriped(offs)]
    h = 0.0625 * (d_k1.T @ xq)
    sq = (h) ** 2
    z = f64(gs) * ((h[np.arange(H)[:, None], runs(n2, H)]) / (np.sqrt(sq + sq[np.arange(H)[:, None], runs(n1, H)] + 0.25)))
    h2 = 0.0625 * ((d_k2.T @ mxq(z, 0, "e4m3")))
    pa = h2[np.arange(H)[:, None], runs(n3, H)]
    return (2.0 * (h2 * pa)) / ((h2) ** 2 + (pa) ** 2 + 0.5)

@@ -1,0 +1,213 @@
+from contextlib import ExitStack
+
+import concourse.mybir as mybir
+
+K, T, S, G, H = 512, 1024, 512, 2048, 512
+FLOPS = 2 * 2 * K * H * S
+P = 128
+PACK = 4
+CHUNKS1 = ((0, 256), (256, 384), (384, 512))
+CHUNKS2 = ((0, 256), (256, 512))
+
+F32 = mybir.dt.float32
+BF16 = mybir.dt.bfloat16
+I32 = mybir.dt.int32
+U32 = mybir.dt.uint32
+U16 = mybir.dt.uint16
+U8 = mybir.dt.uint8
+FP8X4 = mybir.dt.float8_e4m3fn_x4
+ACT = mybir.ActivationFunctionType
+ALU = mybir.AluOpType
+
+
+def tile_picked_codermsharm_none_p_kernel(
+    tc, x_words, x_scales, d_words, d_scales, gs, offs, k1, n1, n2, k2, n3, out
+):
+    nc = tc.nc
+    with ExitStack() as ctx:
+        keep = ctx.enter_context(tc.tile_pool(name="keep", bufs=1))
+        psum = ctx.enter_context(tc.psum_pool(name="psum", bufs=1))
+
+        def sb(name, shape, dtype):
+            return keep.tile(shape, dtype, name=name, align_bytes=64)
+
+        lists = {name: sb("list_" + name, [P, S // 16], U16) for name in ("offs", "k1", "n1", "n2", "k2", "n3")}
+        d_bytes = sb("d_bytes", [P, G], U8)
+        x_bytes = sb("x_bytes", [P, T], U8)
+        d_codes = sb("d_codes", [P, G], U32)
+        x_codes = sb("x_codes", [P, T], U32)
+        gain = sb("gain", [P, PACK], F32)
+        plane1 = sb("plane1", [P, S + H], U8)
+        plane2 = sb("plane2", [P, H], U8)
+        four = sb("four", [P, 1], F32)
+        half = sb("half", [P, 1], F32)
+        c64 = sb("c64", [P, 1], F32)
+
+        nc.gpsimd.memset(four[:], 4.0)
+        nc.gpsimd.memset(c64[:], 64.0)
+        nc.gpsimd.memset(plane1[:].bitcast(I32), 0)
+        nc.gpsimd.memset(plane2[:].bitcast(I32), 0)
+
+        def load_rows(dst, scales):
+            rows = scales[0].bitcast(I32)
+            nc.sync.dma_start(out=dst[:].bitcast(I32), in_=rows.unsqueeze(1).broadcast_to([16, 8, rows.shape[1]]))
+
+        nc.sync.dma_start(lists["k1"][:], k1)
+        load_rows(d_bytes, d_scales)
+        nc.sync.dma_start(lists["offs"][:], offs)
+        load_rows(x_bytes, x_scales)
+        nc.sync.dma_start(out=x_codes[:].bitcast(I32), in_=x_words[0].rearrange("p n t -> p (n t)").bitcast(I32))
+        nc.sync.dma_start(out=d_codes[:].bitcast(I32), in_=d_words[0].rearrange("p n t -> p (n t)").bitcast(I32))
+        nc.sync.dma_start(lists["k2"][:], k2)
+        nc.sync.dma_start(lists["n1"][:], n1)
+        nc.sync.dma_start(out=gain[:], in_=gs.rearrange("(p t) o -> p (t o)", t=PACK))
+        nc.sync.dma_start(lists["n2"][:], n2)
+        nc.sync.dma_start(lists["n3"][:], n3)
+        nc.scalar.activation(out=half[:], in_=four[:], func=ACT.Abs_reciprocal_sqrt)
+
+        def deal(dst, src, run):
+            nc.vector.tensor_copy(
+                out=dst.rearrange("p (t a i) -> p a t i", t=PACK, i=run),
+                in_=src.rearrange("p (a i t) -> p a t i", t=PACK, i=run),
+            )
+
+        def place(plane, staged):
+            for j in range(4):
+                nc.sync.dma_start(out=plane[:].bitcast(I32)[j:P:32, :], in_=staged[:].bitcast(I32)[8 * j : P : 32, :])
+
+        g1_bytes = sb("g1_bytes", [P, H], U8)
+        gx_bytes = sb("gx_bytes", [P, S], U8)
+        staged1 = sb("staged1", [P, S + H], U8)
+        nc.vector.tensor_copy(out=g1_bytes[:], in_=d_bytes[:].indirect(lists["k1"][:]))
+        nc.vector.tensor_copy(out=gx_bytes[:], in_=x_bytes[:].indirect(lists["offs"][:]))
+        deal(staged1[:, S:], g1_bytes[:], 16)
+        nc.vector.tensor_copy(out=staged1[:].bitcast(I32)[:, : S // 4], in_=gx_bytes[:].bitcast(I32))
+        place(plane1, staged1)
+
+
+        gx_codes = sb("gx_codes", [P, S], U32)
+        g1_codes = sb("g1_codes", [P, H], U32)
+        w1_codes = sb("w1_codes", [P, H], U32)
+        nc.vector.tensor_copy(out=gx_codes[:], in_=x_codes[:].indirect(lists["offs"][:]))
+        nc.vector.tensor_copy(out=g1_codes[:], in_=d_codes[:].indirect(lists["k1"][:]))
+        deal(w1_codes[:], g1_codes[:], 4)
+
+        acc1 = [psum.tile([P, S], F32, name=f"acc1_{t}") for t in range(PACK)]
+        for t in range(PACK):
+            nc.tensor.matmul_mx(
+                out=acc1[t][:],
+                lhsT=w1_codes[:, t * P : (t + 1) * P].bitcast(FP8X4),
+                lhsT_scale=plane1[:, S + t * P : S + (t + 1) * P],
+                rhs=gx_codes[:].bitcast(FP8X4),
+                rhs_scale=plane1[:, :S],
+                start=True,
+                stop=True,
+            )
+
+        g2_bytes = sb("g2_bytes", [P, H], U8)
+        staged2 = sb("staged2", [P, H], U8)
+        g2_codes = sb("g2_codes", [P, H], U32)
+        w2_codes = sb("w2_codes", [P, H], U32)
+        nc.vector.tensor_copy(out=g2_bytes[:], in_=d_bytes[:].indirect(lists["k2"][:]))
+        nc.vector.tensor_copy(out=g2_codes[:], in_=d_codes[:].indirect(lists["k2"][:]))
+        deal(staged2[:], g2_bytes[:], 16)
+        deal(w2_codes[:], g2_codes[:], 4)
+        place(plane2, staged2)
+
+        def entries(name, a, b):
+            return lists[name][:, a // 16 : b // 16]
+
+        sq_win = [sb(f"sq_win{t}", [P, S], F32) for t in range(PACK)]
+        h_win = [sb(f"h_win{t}", [P, S], F32) for t in range(PACK)]
+        acc2 = [psum.tile([P, S], F32, name=f"acc2_{t}") for t in range(PACK)]
+        h2_win = [sb(f"h2_win{t}", [P, S], F32) for t in range(PACK)]
+        sq_own = sb("sq_own", [P, PACK, S], F32)
+        ssum = sb("ssum", [P, PACK, S], F32)
+        rinv = sb("rinv", [P, PACK, S], F32)
+        z32 = [sb(f"z32_{c}", [P, PACK, b - a], F32) for c, (a, b) in enumerate(CHUNKS1)]
+        z16 = [sb(f"z16_{c}", [P, b - a, PACK], BF16) for c, (a, b) in enumerate(CHUNKS1)]
+
+        def squares(c, t):
+            a, b = CHUNKS1[c]
+            if c == 0:
+                nc.scalar.activation(out=sq_win[t][:], in_=acc1[t][:], func=ACT.Square, scale=0.0625)
+            nc.scalar.activation(out=sq_own[:, t, a:b], in_=acc1[t][:, a:b], func=ACT.Square, scale=0.0625)
+
+        def norm(c, t):
+            a, b = CHUNKS1[c]
+            nc.vector.tensor_tensor(out=ssum[:, t, a:b], in0=sq_win[t][:].indirect(entries("n1", a, b)), in1=sq_own[:, t, a:b], op=ALU.add)
+            if c == 0:
+                nc.scalar.activation(out=h_win[t][:], in_=acc1[t][:], func=ACT.Copy, scale=gain[:, t : t + 1])
+            nc.scalar.activation(out=rinv[:, t, a:b], in_=ssum[:, t, a:b], func=ACT.Abs_reciprocal_sqrt, scale=256.0, bias=c64[:])
+
+        def scaled(c, t):
+            a, b = CHUNKS1[c]
+            nc.vector.tensor_tensor(out=z32[c][:, t, :], in0=h_win[t][:].indirect(entries("n2", a, b)), in1=rinv[:, t, a:b], op=ALU.mult)
+
+        def weave(c):
+            dst = z16[c][:].rearrange("p (a i) t -> p a t i", i=4)
+            src = z32[c][:].rearrange("p t (a i) -> p a t i", i=4)
+            if c == len(CHUNKS1) - 1:
+                nc.vector.tensor_copy(out=dst, in_=src)
+            else:
+                nc.scalar.copy(out=dst, in_=src)
+
+        def second(c):
+            a, b = CHUNKS1[c]
+            z_codes = sb(f"z_codes{c}", [P, b - a], U32)
+            z_plane = sb(f"z_plane{c}", [P, b - a], U8)
+            nc.vector.quantize_mx(out=z_codes[:].bitcast(FP8X4), scales=z_plane[:], in_=z16[c][:].rearrange("p s t -> p (s t)"))
+            for t in range(PACK):
+                nc.tensor.matmul_mx(
+                    out=acc2[t][:, a:b],
+                    lhsT=w2_codes[:, t * P : (t + 1) * P].bitcast(FP8X4),
+                    lhsT_scale=plane2[:, t * P : (t + 1) * P],
+                    rhs=z_codes[:].bitcast(FP8X4),
+                    rhs_scale=z_plane[:],
+                    start=True,
+                    stop=True,
+                )
+            for t in range(PACK):
+                nc.scalar.activation(out=h2_win[t][:, a:b], in_=acc2[t][:, a:b], func=ACT.Copy, scale=0.0625)
+
+        units = [(c, t) for c in range(len(CHUNKS1)) for t in range(PACK)]
+        squares(*units[0])
+        for i in range(len(units) + 3):
+            if i + 1 < len(units):
+                squares(*units[i + 1])
+            if i < len(units):
+                norm(*units[i])
+            if 1 <= i <= len(units):
+                scaled(*units[i - 1])
+                if units[i - 1][1] == PACK - 1:
+                    weave(units[i - 1][0])
+            if 3 <= i and units[i - 3][1] == PACK - 1:
+                second(units[i - 3][0])
+
+        out_rows = out.rearrange("(p t) s -> t p s", t=PACK)
+        names = ("pa", "pa_sq", "own_sq", "num", "den", "root", "inv", "res")
+        big = {name: sb(name, [P, PACK, S], F32) for name in names}
+
+        def fetch(t, a, b):
+            nc.vector.tensor_copy(out=big["pa"][:, t, a:b], in_=h2_win[t][:].indirect(entries("n3", a, b)))
+            nc.scalar.activation(out=big["own_sq"][:, t, a:b], in_=acc2[t][:, a:b], func=ACT.Square, scale=0.0625)
+            nc.scalar.activation(out=big["pa_sq"][:, t, a:b], in_=big["pa"][:, t, a:b], func=ACT.Square)
+
+        def terms(t, a, b):
+            nc.vector.scalar_tensor_tensor(out=big["num"][:, t, a:b], in0=acc2[t][:, a:b], scalar=0.125, in1=big["pa"][:, t, a:b], op0=ALU.mult, op1=ALU.mult)
+            nc.vector.tensor_tensor(out=big["den"][:, t, a:b], in0=big["pa_sq"][:, t, a:b], in1=big["own_sq"][:, t, a:b], op=ALU.add)
+            nc.scalar.activation(out=big["root"][:, t, a:b], in_=big["den"][:, t, a:b], func=ACT.Abs_reciprocal_sqrt, bias=half[:])
+            nc.scalar.activation(out=big["inv"][:, t, a:b], in_=big["root"][:, t, a:b], func=ACT.Square)
+
+        def finish(t, a, b):
+            nc.vector.tensor_tensor(out=big["res"][:, t, a:b], in0=big["num"][:, t, a:b], in1=big["inv"][:, t, a:b], op=ALU.mult)
+            nc.sync.dma_start(out=out_rows[t][:, a:b], in_=big["res"][:, t, a:b])
+
+        pieces = [(t, a, b) for t in range(PACK - 1) for a, b in CHUNKS2] + [(PACK - 1, a, b) for a, b in CHUNKS1]
+        for i in range(len(pieces) + 2):
+            if i < len(pieces):
+                fetch(*pieces[i])
+            if 1 <= i <= len(pieces):
+                terms(*pieces[i - 1])
+            if 2 <= i:
+                finish(*pieces[i - 2])

@@ -7,7 +7,6 @@ FLOPS = 2 * 2 * K * H * S
 P = 128
 PACK = 4
 CHUNKS1 = ((0, 256), (256, 384), (384, 512))
-CHUNKS2 = ((0, 256), (256, 512))
 
 F32 = mybir.dt.float32
 BF16 = mybir.dt.bfloat16
@@ -28,8 +27,8 @@ def tile_picked_codermsharm_none_p_kernel(
         keep = ctx.enter_context(tc.tile_pool(name="keep", bufs=1))
         psum = ctx.enter_context(tc.psum_pool(name="psum", bufs=1))
 
-        def sb(name, shape, dtype):
-            return keep.tile(shape, dtype, name=name, align_bytes=64)
+        def sb(name, shape, dtype, tag=None):
+            return keep.tile(shape, dtype, name=name, tag=tag or name, align_bytes=64)
 
         lists = {name: sb("list_" + name, [P, S // 16], U16) for name in ("offs", "k1", "n1", "n2", "k2", "n3")}
         d_bytes = sb("d_bytes", [P, G], U8)
@@ -52,10 +51,10 @@ def tile_picked_codermsharm_none_p_kernel(
             rows = scales[0].bitcast(I32)
             nc.sync.dma_start(out=dst[:].bitcast(I32), in_=rows.unsqueeze(1).broadcast_to([16, 8, rows.shape[1]]))
 
-        nc.sync.dma_start(lists["k1"][:], k1)
-        load_rows(d_bytes, d_scales)
         nc.sync.dma_start(lists["offs"][:], offs)
         load_rows(x_bytes, x_scales)
+        nc.sync.dma_start(lists["k1"][:], k1)
+        load_rows(d_bytes, d_scales)
         nc.sync.dma_start(out=x_codes[:].bitcast(I32), in_=x_words[0].rearrange("p n t -> p (n t)").bitcast(I32))
         nc.sync.dma_start(out=d_codes[:].bitcast(I32), in_=d_words[0].rearrange("p n t -> p (n t)").bitcast(I32))
         nc.sync.dma_start(lists["k2"][:], k2)
@@ -78,10 +77,10 @@ def tile_picked_codermsharm_none_p_kernel(
         g1_bytes = sb("g1_bytes", [P, H], U8)
         gx_bytes = sb("gx_bytes", [P, S], U8)
         staged1 = sb("staged1", [P, S + H], U8)
-        nc.vector.tensor_copy(out=g1_bytes[:], in_=d_bytes[:].indirect(lists["k1"][:]))
         nc.vector.tensor_copy(out=gx_bytes[:], in_=x_bytes[:].indirect(lists["offs"][:]))
-        deal(staged1[:, S:], g1_bytes[:], 16)
+        nc.vector.tensor_copy(out=g1_bytes[:], in_=d_bytes[:].indirect(lists["k1"][:]))
         nc.vector.tensor_copy(out=staged1[:].bitcast(I32)[:, : S // 4], in_=gx_bytes[:].bitcast(I32))
+        deal(staged1[:, S:], g1_bytes[:], 16)
         place(plane1, staged1)
 
 
@@ -110,41 +109,50 @@ def tile_picked_codermsharm_none_p_kernel(
         w2_codes = sb("w2_codes", [P, H], U32)
         nc.vector.tensor_copy(out=g2_bytes[:], in_=d_bytes[:].indirect(lists["k2"][:]))
         nc.vector.tensor_copy(out=g2_codes[:], in_=d_codes[:].indirect(lists["k2"][:]))
-        deal(staged2[:], g2_bytes[:], 16)
-        deal(w2_codes[:], g2_codes[:], 4)
+        nc.vector.tensor_copy(
+            out=staged2[:].bitcast(I32).rearrange("p (t a) -> p a t", t=PACK),
+            in_=g2_bytes[:].bitcast(I32).rearrange("p (a t) -> p a t", t=PACK),
+        )
+        nc.vector.tensor_copy(
+            out=w2_codes[:].rearrange("p (t a i) -> p a t i", t=PACK, i=4),
+            in_=g2_codes[:].rearrange("p (a t i) -> p a t i", t=PACK, i=4),
+        )
         place(plane2, staged2)
 
         def entries(name, a, b):
             return lists[name][:, a // 16 : b // 16]
 
-        sq_win = [sb(f"sq_win{t}", [P, S], F32) for t in range(PACK)]
+        wide = [sb(f"wide{t}", [P, 2 * S], F32) for t in range(PACK)]
         h_win = [sb(f"h_win{t}", [P, S], F32) for t in range(PACK)]
         acc2 = [psum.tile([P, S], F32, name=f"acc2_{t}") for t in range(PACK)]
-        h2_win = [sb(f"h2_win{t}", [P, S], F32) for t in range(PACK)]
-        sq_own = sb("sq_own", [P, PACK, S], F32)
-        ssum = sb("ssum", [P, PACK, S], F32)
-        rinv = sb("rinv", [P, PACK, S], F32)
-        z32 = [sb(f"z32_{c}", [P, PACK, b - a], F32) for c, (a, b) in enumerate(CHUNKS1)]
-        z16 = [sb(f"z16_{c}", [P, b - a, PACK], BF16) for c, (a, b) in enumerate(CHUNKS1)]
+        ssum = [sb(f"ssum{t}", [P, S], F32) for t in range(PACK)]
+        rinv = [sb(f"rinv{t}", [P, S], F32) for t in range(PACK)]
+        z32, z16, big = {}, {}, {}
 
-        def squares(c, t):
+        def root(c, t):
             a, b = CHUNKS1[c]
-            if c == 0:
-                nc.scalar.activation(out=sq_win[t][:], in_=acc1[t][:], func=ACT.Square, scale=0.0625)
-            nc.scalar.activation(out=sq_own[:, t, a:b], in_=acc1[t][:, a:b], func=ACT.Square, scale=0.0625)
+            nc.scalar.activation(out=rinv[t][:, a:b], in_=ssum[t][:, a:b], func=ACT.Abs_reciprocal_sqrt, scale=256.0, bias=c64[:])
 
-        def norm(c, t):
-            a, b = CHUNKS1[c]
-            nc.vector.tensor_tensor(out=ssum[:, t, a:b], in0=sq_win[t][:].indirect(entries("n1", a, b)), in1=sq_own[:, t, a:b], op=ALU.add)
-            if c == 0:
-                nc.scalar.activation(out=h_win[t][:], in_=acc1[t][:], func=ACT.Copy, scale=gain[:, t : t + 1])
-            nc.scalar.activation(out=rinv[:, t, a:b], in_=ssum[:, t, a:b], func=ACT.Abs_reciprocal_sqrt, scale=256.0, bias=c64[:])
+        for t in range(PACK):
+            nc.scalar.activation(out=wide[t][:, :S], in_=acc1[t][:], func=ACT.Square, scale=0.0625)
+            nc.scalar.activation(out=wide[t ^ 1][:, S:], in_=acc1[t][:], func=ACT.Square, scale=0.0625)
+        for t in range(PACK):
+            nc.vector.tensor_tensor(out=ssum[t][:], in0=wide[t][:].indirect(lists["n1"][:]), in1=wide[t ^ 1][:, S:], op=ALU.add)
+            root(0, t)
+            nc.scalar.activation(out=h_win[t][:], in_=acc1[t][:], func=ACT.Copy, scale=gain[:, t : t + 1])
+        for c in (1, 2):
+            for t in range(PACK):
+                root(c, t)
 
-        def scaled(c, t):
+        def scaled(c, tag):
             a, b = CHUNKS1[c]
-            nc.vector.tensor_tensor(out=z32[c][:, t, :], in0=h_win[t][:].indirect(entries("n2", a, b)), in1=rinv[:, t, a:b], op=ALU.mult)
+            z32[c] = sb(f"z32_{c}", [P, PACK, b - a], F32, tag)
+            for t in range(PACK):
+                nc.vector.tensor_tensor(out=z32[c][:, t, :], in0=h_win[t][:].indirect(entries("n2", a, b)), in1=rinv[t][:, a:b], op=ALU.mult)
 
         def weave(c):
+            a, b = CHUNKS1[c]
+            z16[c] = sb(f"z16_{c}", [P, b - a, PACK], BF16)
             dst = z16[c][:].rearrange("p (a i) t -> p a t i", i=4)
             src = z32[c][:].rearrange("p t (a i) -> p a t i", i=4)
             if c == len(CHUNKS1) - 1:
@@ -152,12 +160,23 @@ def tile_picked_codermsharm_none_p_kernel(
             else:
                 nc.scalar.copy(out=dst, in_=src)
 
+        def own_rest(t):
+            a = CHUNKS1[-1][0]
+            nc.scalar.activation(out=big["own"][:, t, a:], in_=acc2[t][:, a:], func=ACT.Square, scale=0.0625)
+
         def second(c):
             a, b = CHUNKS1[c]
             z_codes = sb(f"z_codes{c}", [P, b - a], U32)
             z_plane = sb(f"z_plane{c}", [P, b - a], U8)
             nc.vector.quantize_mx(out=z_codes[:].bitcast(FP8X4), scales=z_plane[:], in_=z16[c][:].rearrange("p s t -> p (s t)"))
-            for t in range(PACK):
+            if c == len(CHUNKS1) - 1:
+                big["own"] = sb("own_sq", [P, PACK, S], F32, "z16_2")
+                for t in (0, 1):
+                    nc.gpsimd.tensor_tensor(out=big["own"][:, t, :a], in0=wide[t][:, :a], in1=wide[t][:, :a], op=ALU.mult)
+                for t in (2, 3):
+                    nc.vector.scalar_tensor_tensor(out=big["own"][:, t, :a], in0=acc2[t][:, :a], scalar=0.0625, in1=wide[t][:, :a], op0=ALU.mult, op1=ALU.mult)
+            order = (2, 3, 0, 1) if c == 1 else range(PACK)
+            for t in order:
                 nc.tensor.matmul_mx(
                     out=acc2[t][:, a:b],
                     lhsT=w2_codes[:, t * P : (t + 1) * P].bitcast(FP8X4),
@@ -167,47 +186,61 @@ def tile_picked_codermsharm_none_p_kernel(
                     start=True,
                     stop=True,
                 )
-            for t in range(PACK):
-                nc.scalar.activation(out=h2_win[t][:, a:b], in_=acc2[t][:, a:b], func=ACT.Copy, scale=0.0625)
+            for t in order:
+                nc.scalar.activation(out=wide[t][:, a:b], in_=acc2[t][:, a:b], func=ACT.Copy, scale=0.0625)
+                if c == 2 and t % 2 == 1:
+                    own_rest(t // 2)
 
-        units = [(c, t) for c in range(len(CHUNKS1)) for t in range(PACK)]
-        squares(*units[0])
-        for i in range(len(units) + 3):
-            if i + 1 < len(units):
-                squares(*units[i + 1])
-            if i < len(units):
-                norm(*units[i])
-            if 1 <= i <= len(units):
-                scaled(*units[i - 1])
-                if units[i - 1][1] == PACK - 1:
-                    weave(units[i - 1][0])
-            if 3 <= i and units[i - 3][1] == PACK - 1:
-                second(units[i - 3][0])
+        scaled(0, None)
+        weave(0)
+        scaled(1, None)
+        weave(1)
+        second(0)
+        scaled(2, "z16_0")
+        second(1)
+        weave(2)
+        second(2)
 
-        out_rows = out.rearrange("(p t) s -> t p s", t=PACK)
-        names = ("pa", "pa_sq", "own_sq", "num", "den", "root", "inv", "res")
-        big = {name: sb(name, [P, PACK, S], F32) for name in names}
+        out_rows = out.rearrange("(a t i) s -> t a i s", t=PACK, i=4)
+        HALF = S // 2
+        pa = sb("pa", [P, PACK, S], F32)
+        inv = sb("inv", [P, PACK, S], F32)
+        pieces = [(t, a, a + HALF) for t in range(PACK) for a in (0, HALF)]
 
-        def fetch(t, a, b):
-            nc.vector.tensor_copy(out=big["pa"][:, t, a:b], in_=h2_win[t][:].indirect(entries("n3", a, b)))
-            nc.scalar.activation(out=big["own_sq"][:, t, a:b], in_=acc2[t][:, a:b], func=ACT.Square, scale=0.0625)
-            nc.scalar.activation(out=big["pa_sq"][:, t, a:b], in_=big["pa"][:, t, a:b], func=ACT.Square)
+        def made(name, i, tag=None):
+            big[name, i] = sb(f"{name}{i}", [P, HALF], F32, tag)
+            return big[name, i][:]
 
-        def terms(t, a, b):
-            nc.vector.scalar_tensor_tensor(out=big["num"][:, t, a:b], in0=acc2[t][:, a:b], scalar=0.125, in1=big["pa"][:, t, a:b], op0=ALU.mult, op1=ALU.mult)
-            nc.vector.tensor_tensor(out=big["den"][:, t, a:b], in0=big["pa_sq"][:, t, a:b], in1=big["own_sq"][:, t, a:b], op=ALU.add)
-            nc.scalar.activation(out=big["root"][:, t, a:b], in_=big["den"][:, t, a:b], func=ACT.Abs_reciprocal_sqrt, bias=half[:])
-            nc.scalar.activation(out=big["inv"][:, t, a:b], in_=big["root"][:, t, a:b], func=ACT.Square)
+        def denominator(i):
+            t, a, b = pieces[i]
+            nc.scalar.activation(out=made("pa_sq", i, f"den{i - 3}" if i >= 3 else None), in_=pa[:, t, a:b], func=ACT.Square)
+            nc.gpsimd.tensor_tensor(out=made("den", i), in0=big["pa_sq", i][:], in1=big["own"][:, t, a:b], op=ALU.add)
 
-        def finish(t, a, b):
-            nc.vector.tensor_tensor(out=big["res"][:, t, a:b], in0=big["num"][:, t, a:b], in1=big["inv"][:, t, a:b], op=ALU.mult)
-            nc.sync.dma_start(out=out_rows[t][:, a:b], in_=big["res"][:, t, a:b])
+        def root2(i):
+            nc.scalar.activation(out=made("root", i), in_=big["den", i][:], func=ACT.Abs_reciprocal_sqrt, bias=half[:])
 
-        pieces = [(t, a, b) for t in range(PACK - 1) for a, b in CHUNKS2] + [(PACK - 1, a, b) for a, b in CHUNKS1]
-        for i in range(len(pieces) + 2):
-            if i < len(pieces):
-                fetch(*pieces[i])
-            if 1 <= i <= len(pieces):
-                terms(*pieces[i - 1])
-            if 2 <= i:
-                finish(*pieces[i - 2])
+        def inverse(i):
+            t, a, b = pieces[i]
+            nc.scalar.activation(out=inv[:, t, a:b], in_=big["root", i][:], func=ACT.Square)
+
+        for t, a, b in pieces:
+            nc.vector.tensor_copy(out=pa[:, t, a:b], in_=wide[t][:].indirect(entries("n3", a, b)))
+        for i in range(3):
+            denominator(i)
+            if i < 2:
+                own_rest(2 + i)
+        for i in range(len(pieces)):
+            root2(i)
+            if i + 3 < len(pieces):
+                denominator(i + 3)
+            if i >= 1:
+                inverse(i - 1)
+        inverse(len(pieces) - 1)
+        num = sb("num", [P, PACK, S], F32, "wide3")
+        for t in range(PACK):
+            nc.vector.scalar_tensor_tensor(out=num[:, t, :], in0=acc2[t][:], scalar=0.125, in1=pa[:, t, :], op0=ALU.mult, op1=ALU.mult)
+        res = sb("res", [P, PACK, S], F32)
+        for t in range(PACK):
+            for a, b in ((0, S),) if t < PACK - 1 else ((0, HALF), (HALF, 384), (384, S)):
+                nc.vector.tensor_tensor(out=res[:, t, a:b], in0=num[:, t, a:b], in1=inv[:, t, a:b], op=ALU.mult)
+                nc.sync.dma_start(out=out_rows[t][:, :, a:b], in_=res[:, t, a:b])

@@ -56,10 +56,10 @@ def tile_picked_codermsharm_none_p_kernel(
         nc.sync.dma_start(lists["k1"][:], k1)
         load_rows(d_bytes, d_scales)
         nc.sync.dma_start(out=x_codes[:].bitcast(I32), in_=x_words[0].rearrange("p n t -> p (n t)").bitcast(I32))
+        nc.sync.dma_start(lists["n1"][:], n1)
         nc.sync.dma_start(out=d_codes[:].bitcast(I32), in_=d_words[0].rearrange("p n t -> p (n t)").bitcast(I32))
         nc.sync.dma_start(lists["k2"][:], k2)
-        nc.sync.dma_start(lists["n1"][:], n1)
-        nc.sync.dma_start(out=gain[:], in_=gs.rearrange("(p t) o -> p (t o)", t=PACK))
+        nc.gpsimd.dma_start(out=gain[:], in_=gs.rearrange("(p t) o -> p (t o)", t=PACK))
         nc.sync.dma_start(lists["n2"][:], n2)
         nc.sync.dma_start(lists["n3"][:], n3)
         nc.scalar.activation(out=half[:], in_=four[:], func=ACT.Abs_reciprocal_sqrt)
@@ -92,7 +92,8 @@ def tile_picked_codermsharm_none_p_kernel(
         deal(w1_codes[:], g1_codes[:], 4)
 
         acc1 = [psum.tile([P, S], F32, name=f"acc1_{t}") for t in range(PACK)]
-        for t in range(PACK):
+        HALF = S // 2
+        for t in (0, 3, 1, 2):
             nc.tensor.matmul_mx(
                 out=acc1[t][:],
                 lhsT=w1_codes[:, t * P : (t + 1) * P].bitcast(FP8X4),
@@ -110,45 +111,56 @@ def tile_picked_codermsharm_none_p_kernel(
         nc.vector.tensor_copy(out=g2_bytes[:], in_=d_bytes[:].indirect(lists["k2"][:]))
         nc.vector.tensor_copy(out=g2_codes[:], in_=d_codes[:].indirect(lists["k2"][:]))
         nc.vector.tensor_copy(
-            out=staged2[:].bitcast(I32).rearrange("p (t a) -> p a t", t=PACK),
-            in_=g2_bytes[:].bitcast(I32).rearrange("p (a t) -> p a t", t=PACK),
-        )
-        nc.vector.tensor_copy(
-            out=w2_codes[:].rearrange("p (t a i) -> p a t i", t=PACK, i=4),
-            in_=g2_codes[:].rearrange("p (a t i) -> p a t i", t=PACK, i=4),
+            out=staged2[:].bitcast(I32).rearrange("p (t r i) -> p r t i", t=PACK, i=4),
+            in_=g2_bytes[:].bitcast(I32).rearrange("p (r t i) -> p r t i", t=PACK, i=4),
         )
         place(plane2, staged2)
+        g2_runs = g2_codes[:].bitcast(I32).rearrange("p (r t i) -> p t r i", t=PACK, i=16)
+        for t in range(PACK):
+            nc.sync.dma_start(
+                out=w2_codes[:, t * P : (t + 1) * P].bitcast(I32).rearrange("p (r i) -> p r i", i=16),
+                in_=g2_runs[:, t],
+            )
 
         def entries(name, a, b):
             return lists[name][:, a // 16 : b // 16]
 
-        wide = [sb(f"wide{t}", [P, 2 * S], F32) for t in range(PACK)]
+        wide = [sb(f"wide{t}", [P, 2 * S if t else S], F32) for t in range(PACK)]
+        twin_last = sb("twin_last", [P, S], F32)
+        twin = [wide[t + 1][:, S:] for t in range(PACK - 1)] + [twin_last[:]]
         h_win = [sb(f"h_win{t}", [P, S], F32) for t in range(PACK)]
         acc2 = [psum.tile([P, S], F32, name=f"acc2_{t}") for t in range(PACK)]
         ssum = [sb(f"ssum{t}", [P, S], F32) for t in range(PACK)]
-        rinv = [sb(f"rinv{t}", [P, S], F32) for t in range(PACK)]
         z32, z16, big = {}, {}, {}
+        rinv = {c: sb(f"rinv{c}", [P, PACK, CHUNKS1[c][1] - CHUNKS1[c][0]], F32) for c in (0, 1)}
 
         def root(c, t):
             a, b = CHUNKS1[c]
-            nc.scalar.activation(out=rinv[t][:, a:b], in_=ssum[t][:, a:b], func=ACT.Abs_reciprocal_sqrt, scale=256.0, bias=c64[:])
+            nc.scalar.activation(out=rinv[c][:, t, :], in_=ssum[t][:, a:b], func=ACT.Abs_reciprocal_sqrt, scale=256.0, bias=c64[:])
 
+        def square(dst, t):
+            nc.scalar.activation(out=dst, in_=acc1[t][:], func=ACT.Square, scale=0.0625)
+
+        square(wide[0][:], 0)
+        nc.gpsimd.tensor_scalar(out=twin[0], in0=wide[0][:], scalar1=1.0, scalar2=0.0, op0=ALU.mult, op1=ALU.add)
+        square(wide[3][:, :S], 3)
+        nc.sync.dma_start(out=twin[3], in_=wide[3][:, :S])
+        for t in (1, 2):
+            square(wide[t][:, :S], t)
+            square(twin[t], t)
         for t in range(PACK):
-            nc.scalar.activation(out=wide[t][:, :S], in_=acc1[t][:], func=ACT.Square, scale=0.0625)
-            nc.scalar.activation(out=wide[t ^ 1][:, S:], in_=acc1[t][:], func=ACT.Square, scale=0.0625)
-        for t in range(PACK):
-            nc.vector.tensor_tensor(out=ssum[t][:], in0=wide[t][:].indirect(lists["n1"][:]), in1=wide[t ^ 1][:, S:], op=ALU.add)
+            for a, b in ((0, S),) if t else ((0, HALF), (HALF, S)):
+                nc.vector.tensor_tensor(out=ssum[t][:, a:b], in0=wide[t][:].indirect(entries("n1", a, b)), in1=twin[t][:, a:b], op=ALU.add)
             root(0, t)
             nc.scalar.activation(out=h_win[t][:], in_=acc1[t][:], func=ACT.Copy, scale=gain[:, t : t + 1])
-        for c in (1, 2):
-            for t in range(PACK):
-                root(c, t)
+        for t in range(PACK):
+            root(1, t)
 
         def scaled(c, tag):
             a, b = CHUNKS1[c]
             z32[c] = sb(f"z32_{c}", [P, PACK, b - a], F32, tag)
             for t in range(PACK):
-                nc.vector.tensor_tensor(out=z32[c][:, t, :], in0=h_win[t][:].indirect(entries("n2", a, b)), in1=rinv[t][:, a:b], op=ALU.mult)
+                nc.vector.tensor_tensor(out=z32[c][:, t, :], in0=h_win[t][:].indirect(entries("n2", a, b)), in1=rinv[c][:, t, :], op=ALU.mult)
 
         def weave(c):
             a, b = CHUNKS1[c]
@@ -193,6 +205,9 @@ def tile_picked_codermsharm_none_p_kernel(
 
         scaled(0, None)
         weave(0)
+        rinv[2] = sb("rinv2", [P, PACK, CHUNKS1[2][1] - CHUNKS1[2][0]], F32, "z32_0")
+        for t in range(PACK):
+            root(2, t)
         scaled(1, None)
         weave(1)
         second(0)
@@ -201,8 +216,7 @@ def tile_picked_codermsharm_none_p_kernel(
         weave(2)
         second(2)
 
-        out_rows = out.rearrange("(a t i) s -> t a i s", t=PACK, i=4)
-        HALF = S // 2
+        out_rows = out.rearrange("(r t i) s -> t r i s", t=PACK, i=16)
         pa = sb("pa", [P, PACK, S], F32)
         inv = sb("inv", [P, PACK, S], F32)
         pieces = [(t, a, a + HALF) for t in range(PACK) for a in (0, HALF)]

@@ -111,16 +111,14 @@ def tile_picked_codermsharm_none_p_kernel(
         nc.vector.tensor_copy(out=g2_bytes[:], in_=d_bytes[:].indirect(lists["k2"][:]))
         nc.vector.tensor_copy(out=g2_codes[:], in_=d_codes[:].indirect(lists["k2"][:]))
         nc.vector.tensor_copy(
-            out=staged2[:].bitcast(I32).rearrange("p (t r i) -> p r t i", t=PACK, i=4),
-            in_=g2_bytes[:].bitcast(I32).rearrange("p (r t i) -> p r t i", t=PACK, i=4),
+            out=staged2[:].bitcast(I32).rearrange("p (t a) -> p a t", t=PACK),
+            in_=g2_bytes[:].bitcast(I32).rearrange("p (a t) -> p a t", t=PACK),
+        )
+        nc.vector.tensor_copy(
+            out=w2_codes[:].rearrange("p (t a i) -> p a t i", t=PACK, i=4),
+            in_=g2_codes[:].rearrange("p (a t i) -> p a t i", t=PACK, i=4),
         )
         place(plane2, staged2)
-        g2_runs = g2_codes[:].bitcast(I32).rearrange("p (r t i) -> p t r i", t=PACK, i=16)
-        for t in range(PACK):
-            nc.sync.dma_start(
-                out=w2_codes[:, t * P : (t + 1) * P].bitcast(I32).rearrange("p (r i) -> p r i", i=16),
-                in_=g2_runs[:, t],
-            )
 
         def entries(name, a, b):
             return lists[name][:, a // 16 : b // 16]
@@ -216,7 +214,7 @@ def tile_picked_codermsharm_none_p_kernel(
         weave(2)
         second(2)
 
-        out_rows = out.rearrange("(r t i) s -> t r i s", t=PACK, i=16)
+        out_rows = out.rearrange("(a t i) s -> t a i s", t=PACK, i=4)
         pa = sb("pa", [P, PACK, S], F32)
         inv = sb("inv", [P, PACK, S], F32)
         pieces = [(t, a, a + HALF) for t in range(PACK) for a in (0, HALF)]

from contextlib import ExitStack

import concourse.mybir as mybir

K, T, S, G, H = 512, 1024, 512, 2048, 512
FLOPS = 2 * 2 * K * H * S
P = 128
PACK = 4
CHUNKS1 = ((0, 256), (256, 384), (384, 512))

F32 = mybir.dt.float32
BF16 = mybir.dt.bfloat16
I32 = mybir.dt.int32
U32 = mybir.dt.uint32
U16 = mybir.dt.uint16
U8 = mybir.dt.uint8
FP8X4 = mybir.dt.float8_e4m3fn_x4
ACT = mybir.ActivationFunctionType
ALU = mybir.AluOpType


def tile_picked_codermsharm_none_p_kernel(
    tc, x_words, x_scales, d_words, d_scales, gs, offs, k1, n1, n2, k2, n3, out
):
    nc = tc.nc
    with ExitStack() as ctx:
        keep = ctx.enter_context(tc.tile_pool(name="keep", bufs=1))
        psum = ctx.enter_context(tc.psum_pool(name="psum", bufs=1))

        def sb(name, shape, dtype, tag=None):
            return keep.tile(shape, dtype, name=name, tag=tag or name, align_bytes=64)

        lists = {name: sb("list_" + name, [P, S // 16], U16) for name in ("offs", "k1", "n1", "n2", "k2", "n3")}
        d_bytes = sb("d_bytes", [P, G], U8)
        x_bytes = sb("x_bytes", [P, T], U8)
        d_codes = sb("d_codes", [P, G], U32)
        x_codes = sb("x_codes", [P, T], U32)
        gain = sb("gain", [P, PACK], F32)
        plane1 = sb("plane1", [P, S + H], U8)
        plane2 = sb("plane2", [P, H], U8)
        four = sb("four", [P, 1], F32)
        half = sb("half", [P, 1], F32)
        c64 = sb("c64", [P, 1], F32)

        nc.gpsimd.memset(four[:], 4.0)
        nc.gpsimd.memset(c64[:], 64.0)
        nc.gpsimd.memset(plane1[:].bitcast(I32), 0)
        nc.gpsimd.memset(plane2[:].bitcast(I32), 0)

        def load_rows(dst, scales):
            rows = scales[0].bitcast(I32)
            nc.sync.dma_start(out=dst[:].bitcast(I32), in_=rows.unsqueeze(1).broadcast_to([16, 8, rows.shape[1]]))

        nc.sync.dma_start(lists["offs"][:], offs)
        load_rows(x_bytes, x_scales)
        nc.sync.dma_start(lists["k1"][:], k1)
        load_rows(d_bytes, d_scales)
        nc.sync.dma_start(out=x_codes[:].bitcast(I32), in_=x_words[0].rearrange("p n t -> p (n t)").bitcast(I32))
        nc.sync.dma_start(lists["n1"][:], n1)
        nc.sync.dma_start(out=d_codes[:].bitcast(I32), in_=d_words[0].rearrange("p n t -> p (n t)").bitcast(I32))
        nc.sync.dma_start(lists["k2"][:], k2)
        nc.gpsimd.dma_start(out=gain[:], in_=gs.rearrange("(p t) o -> p (t o)", t=PACK))
        nc.sync.dma_start(lists["n2"][:], n2)
        nc.sync.dma_start(lists["n3"][:], n3)
        nc.scalar.activation(out=half[:], in_=four[:], func=ACT.Abs_reciprocal_sqrt)

        def deal(dst, src, run):
            nc.vector.tensor_copy(
                out=dst.rearrange("p (t a i) -> p a t i", t=PACK, i=run),
                in_=src.rearrange("p (a i t) -> p a t i", t=PACK, i=run),
            )

        def place(plane, staged):
            for j in range(4):
                nc.sync.dma_start(out=plane[:].bitcast(I32)[j:P:32, :], in_=staged[:].bitcast(I32)[8 * j : P : 32, :])

        g1_bytes = sb("g1_bytes", [P, H], U8)
        gx_bytes = sb("gx_bytes", [P, S], U8)
        staged1 = sb("staged1", [P, S + H], U8)
        nc.vector.tensor_copy(out=gx_bytes[:], in_=x_bytes[:].indirect(lists["offs"][:]))
        nc.vector.tensor_copy(out=g1_bytes[:], in_=d_bytes[:].indirect(lists["k1"][:]))
        nc.vector.tensor_copy(out=staged1[:].bitcast(I32)[:, : S // 4], in_=gx_bytes[:].bitcast(I32))
        deal(staged1[:, S:], g1_bytes[:], 16)
        place(plane1, staged1)


        gx_codes = sb("gx_codes", [P, S], U32)
        g1_codes = sb("g1_codes", [P, H], U32)
        w1_codes = sb("w1_codes", [P, H], U32)
        nc.vector.tensor_copy(out=gx_codes[:], in_=x_codes[:].indirect(lists["offs"][:]))
        nc.vector.tensor_copy(out=g1_codes[:], in_=d_codes[:].indirect(lists["k1"][:]))
        deal(w1_codes[:], g1_codes[:], 4)

        acc1 = [psum.tile([P, S], F32, name=f"acc1_{t}") for t in range(PACK)]
        HALF = S // 2
        for t in (0, 3, 1, 2):
            nc.tensor.matmul_mx(
                out=acc1[t][:],
                lhsT=w1_codes[:, t * P : (t + 1) * P].bitcast(FP8X4),
                lhsT_scale=plane1[:, S + t * P : S + (t + 1) * P],
                rhs=gx_codes[:].bitcast(FP8X4),
                rhs_scale=plane1[:, :S],
                start=True,
                stop=True,
            )

        g2_bytes = sb("g2_bytes", [P, H], U8)
        staged2 = sb("staged2", [P, H], U8)
        g2_codes = sb("g2_codes", [P, H], U32)
        w2_codes = sb("w2_codes", [P, H], U32)
        nc.vector.tensor_copy(out=g2_bytes[:], in_=d_bytes[:].indirect(lists["k2"][:]))
        nc.vector.tensor_copy(out=g2_codes[:], in_=d_codes[:].indirect(lists["k2"][:]))
        nc.vector.tensor_copy(
            out=staged2[:].bitcast(I32).rearrange("p (t a) -> p a t", t=PACK),
            in_=g2_bytes[:].bitcast(I32).rearrange("p (a t) -> p a t", t=PACK),
        )
        nc.vector.tensor_copy(
            out=w2_codes[:].rearrange("p (t a i) -> p a t i", t=PACK, i=4),
            in_=g2_codes[:].rearrange("p (a t i) -> p a t i", t=PACK, i=4),
        )
        place(plane2, staged2)

        def entries(name, a, b):
            return lists[name][:, a // 16 : b // 16]

        wide = [sb(f"wide{t}", [P, 2 * S if t else S], F32) for t in range(PACK)]
        twin_last = sb("twin_last", [P, S], F32)
        twin = [wide[t + 1][:, S:] for t in range(PACK - 1)] + [twin_last[:]]
        h_win = [sb(f"h_win{t}", [P, S], F32) for t in range(PACK)]
        acc2 = [psum.tile([P, S], F32, name=f"acc2_{t}") for t in range(PACK)]
        ssum = [sb(f"ssum{t}", [P, S], F32) for t in range(PACK)]
        z32, z16, big = {}, {}, {}
        rinv = {c: sb(f"rinv{c}", [P, PACK, CHUNKS1[c][1] - CHUNKS1[c][0]], F32) for c in (0, 1)}

        def root(c, t):
            a, b = CHUNKS1[c]
            nc.scalar.activation(out=rinv[c][:, t, :], in_=ssum[t][:, a:b], func=ACT.Abs_reciprocal_sqrt, scale=256.0, bias=c64[:])

        def square(dst, t):
            nc.scalar.activation(out=dst, in_=acc1[t][:], func=ACT.Square, scale=0.0625)

        square(wide[0][:], 0)
        nc.gpsimd.tensor_scalar(out=twin[0], in0=wide[0][:], scalar1=1.0, scalar2=0.0, op0=ALU.mult, op1=ALU.add)
        square(wide[3][:, :S], 3)
        nc.sync.dma_start(out=twin[3], in_=wide[3][:, :S])
        for t in (1, 2):
            square(wide[t][:, :S], t)
            square(twin[t], t)
        for t in range(PACK):
            for a, b in ((0, S),) if t else ((0, HALF), (HALF, S)):
                nc.vector.tensor_tensor(out=ssum[t][:, a:b], in0=wide[t][:].indirect(entries("n1", a, b)), in1=twin[t][:, a:b], op=ALU.add)
            root(0, t)
            nc.scalar.activation(out=h_win[t][:], in_=acc1[t][:], func=ACT.Copy, scale=gain[:, t : t + 1])
        for t in range(PACK):
            root(1, t)

        def scaled(c, tag):
            a, b = CHUNKS1[c]
            z32[c] = sb(f"z32_{c}", [P, PACK, b - a], F32, tag)
            for t in range(PACK):
                nc.vector.tensor_tensor(out=z32[c][:, t, :], in0=h_win[t][:].indirect(entries("n2", a, b)), in1=rinv[c][:, t, :], op=ALU.mult)

        def weave(c):
            a, b = CHUNKS1[c]
            z16[c] = sb(f"z16_{c}", [P, b - a, PACK], BF16)
            dst = z16[c][:].rearrange("p (a i) t -> p a t i", i=4)
            src = z32[c][:].rearrange("p t (a i) -> p a t i", i=4)
            if c == len(CHUNKS1) - 1:
                nc.vector.tensor_copy(out=dst, in_=src)
            else:
                nc.scalar.copy(out=dst, in_=src)

        def own_rest(t):
            a = CHUNKS1[-1][0]
            nc.scalar.activation(out=big["own"][:, t, a:], in_=acc2[t][:, a:], func=ACT.Square, scale=0.0625)

        def second(c):
            a, b = CHUNKS1[c]
            z_codes = sb(f"z_codes{c}", [P, b - a], U32)
            z_plane = sb(f"z_plane{c}", [P, b - a], U8)
            nc.vector.quantize_mx(out=z_codes[:].bitcast(FP8X4), scales=z_plane[:], in_=z16[c][:].rearrange("p s t -> p (s t)"))
            if c == len(CHUNKS1) - 1:
                big["own"] = sb("own_sq", [P, PACK, S], F32, "z16_2")
                for t in (0, 1):
                    nc.gpsimd.tensor_tensor(out=big["own"][:, t, :a], in0=wide[t][:, :a], in1=wide[t][:, :a], op=ALU.mult)
                for t in (2, 3):
                    nc.vector.scalar_tensor_tensor(out=big["own"][:, t, :a], in0=acc2[t][:, :a], scalar=0.0625, in1=wide[t][:, :a], op0=ALU.mult, op1=ALU.mult)
            order = (2, 3, 0, 1) if c == 1 else range(PACK)
            for t in order:
                nc.tensor.matmul_mx(
                    out=acc2[t][:, a:b],
                    lhsT=w2_codes[:, t * P : (t + 1) * P].bitcast(FP8X4),
                    lhsT_scale=plane2[:, t * P : (t + 1) * P],
                    rhs=z_codes[:].bitcast(FP8X4),
                    rhs_scale=z_plane[:],
                    start=True,
                    stop=True,
                )
            for t in order:
                nc.scalar.activation(out=wide[t][:, a:b], in_=acc2[t][:, a:b], func=ACT.Copy, scale=0.0625)
                if c == 2 and t % 2 == 1:
                    own_rest(t // 2)

        scaled(0, None)
        weave(0)
        rinv[2] = sb("rinv2", [P, PACK, CHUNKS1[2][1] - CHUNKS1[2][0]], F32, "z32_0")
        for t in range(PACK):
            root(2, t)
        scaled(1, None)
        weave(1)
        second(0)
        scaled(2, "z16_0")
        second(1)
        weave(2)
        second(2)

        out_rows = out.rearrange("(a t i) s -> t a i s", t=PACK, i=4)
        pa = sb("pa", [P, PACK, S], F32)
        inv = sb("inv", [P, PACK, S], F32)
        pieces = [(t, a, a + HALF) for t in range(PACK) for a in (0, HALF)]

        def made(name, i, tag=None):
            big[name, i] = sb(f"{name}{i}", [P, HALF], F32, tag)
            return big[name, i][:]

        def denominator(i):
            t, a, b = pieces[i]
            nc.scalar.activation(out=made("pa_sq", i, f"den{i - 3}" if i >= 3 else None), in_=pa[:, t, a:b], func=ACT.Square)
            nc.gpsimd.tensor_tensor(out=made("den", i), in0=big["pa_sq", i][:], in1=big["own"][:, t, a:b], op=ALU.add)

        def root2(i):
            nc.scalar.activation(out=made("root", i), in_=big["den", i][:], func=ACT.Abs_reciprocal_sqrt, bias=half[:])

        def inverse(i):
            t, a, b = pieces[i]
            nc.scalar.activation(out=inv[:, t, a:b], in_=big["root", i][:], func=ACT.Square)

        for t, a, b in pieces:
            nc.vector.tensor_copy(out=pa[:, t, a:b], in_=wide[t][:].indirect(entries("n3", a, b)))
        for i in range(3):
            denominator(i)
            if i < 2:
                own_rest(2 + i)
        for i in range(len(pieces)):
            root2(i)
            if i + 3 < len(pieces):
                denominator(i + 3)
            if i >= 1:
                inverse(i - 1)
        inverse(len(pieces) - 1)
        num = sb("num", [P, PACK, S], F32, "wide3")
        for t in range(PACK):
            nc.vector.scalar_tensor_tensor(out=num[:, t, :], in0=acc2[t][:], scalar=0.125, in1=pa[:, t, :], op0=ALU.mult, op1=ALU.mult)
        res = sb("res", [P, PACK, S], F32)
        for t in range(PACK):
            for a, b in ((0, S),) if t < PACK - 1 else ((0, HALF), (HALF, 384), (384, S)):
                nc.vector.tensor_tensor(out=res[:, t, a:b], in0=num[:, t, a:b], in1=inv[:, t, a:b], op=ALU.mult)
                nc.sync.dma_start(out=out_rows[t][:, :, a:b], in_=res[:, t, a:b])
